import numpy as np
import ml_dtypes


def mxq(x, axis, fmt="e4m3"):
    dtype, down = {"e4m3": (ml_dtypes.float8_e4m3fn, 7), "e5m2": (ml_dtypes.float8_e5m2, 14)}[fmt]
    v = np.moveaxis(np.asarray(x, np.float32).astype(ml_dtypes.bfloat16).astype(np.float64), axis, -1)
    blocks = v.reshape(v.shape[:-1] + (-1, 32))
    amax = np.abs(blocks).max(-1, keepdims=True)
    byte = np.maximum(np.where(amax > 0, np.frexp(amax)[1] - 1 + 127, 0) - down, 1)
    scale = np.exp2(byte - 127.0)
    codes = (blocks / scale).astype(np.float32).astype(dtype).astype(np.float64)
    return np.moveaxis((codes * scale).reshape(v.shape), -1, axis)


WIDE = False


def mx_kscale(k):
    if not WIDE:
        return np.ones(k)
    levels = np.array([30, -30])
    if k % 512:
        return np.exp2(np.random.permutation(np.resize(levels, k // 32))).repeat(32)
    a = np.empty((k // 512, 16))
    for p in range(k // 512):
        a[p, :8] = np.random.permutation(np.resize(levels, 8))
        for g in range(8):
            far = levels[np.abs(levels - a[p, g]) >= 10]
            a[p, g + 8] = far[np.random.randint(len(far))]
    return np.exp2(a.ravel()).repeat(32)


def f64(x):
    return np.asarray(x).astype(np.float64)


def striped(idx):
    return np.tile(np.asarray(idx).reshape(-1, 16).T, (8, 1)).astype(np.uint16)


def unstriped(offs):
    return offs[:16].T.reshape(-1).astype(np.int64)


E2M1 = np.array([0.0, 0.5, 1.0, 1.5, 2.0, 3.0, 4.0, 6.0, -0.0, -0.5, -1.0, -1.5, -2.0, -3.0, -4.0, -6.0])


def pack_weight(w, fmt):
    k, n = w.shape
    w = f64(np.asarray(w, np.float32).astype(ml_dtypes.bfloat16)).reshape(k // 32, 32, n)
    amax = np.abs(w).max(1)
    if fmt in ("e4m3", "e5m2"):
        byte = np.frexp(amax)[1] - 1 + 127 - (7 if fmt == "e4m3" else 14)
    else:
        mant, ex = np.frexp(amax / 6.0)
        byte = np.where(mant > 0.5, ex, ex - 1) + 127
    byte = np.clip(np.where(amax > 0, byte, 1), 1, 254)
    scaled = (w * np.exp2(127.0 - byte)[:, None, :]).reshape(k, n).astype(np.float32)
    by_word = np.ascontiguousarray(scaled.reshape(k // 512, 128, 4, n).transpose(0, 1, 3, 2))
    if fmt in ("e4m3", "e5m2"):
        words = by_word.astype(ml_dtypes.float8_e4m3fn if fmt == "e4m3" else ml_dtypes.float8_e5m2).view(np.uint8)
    else:
        c = by_word.astype(ml_dtypes.float4_e2m1fn).view(np.uint8) & 0xF
        words = (c[..., 0::2] | (c[..., 1::2] << 4)).reshape(k // 512, 128, 2 * n)
    return np.ascontiguousarray(words), np.ascontiguousarray(byte.astype(np.uint8).reshape(k // 512, 16, n))


def unpack_weight(words, scales, fmt):
    g, _, n = scales.shape
    words = np.ascontiguousarray(words).reshape(g, 128, n, -1)
    if fmt in ("e4m3", "e5m2"):
        vals = words.view(ml_dtypes.float8_e4m3fn if fmt == "e4m3" else ml_dtypes.float8_e5m2).astype(np.float64)
    else:
        nib = np.empty((g, 128, n, 4), np.uint8)
        nib[..., 0::2] = words & 0xF
        nib[..., 1::2] = words >> 4
        vals = E2M1[nib]
    vals = vals * np.repeat(np.exp2(scales.astype(np.float64) - 127.0), 8, axis=1)[..., None]
    return vals.transpose(0, 1, 3, 2).reshape(g * 512, n)


K, T, Z, J, R, N, L, E = 512, 1024, 1024, 256, 512, 256, 512, 1024


def setup_inputs():
    n = np.random.standard_normal
    idx = np.random.permutation(T)[:J]
    idx2 = np.random.permutation(Z)[:J]
    idx3 = np.random.permutation(E)[:J]
    fk = mx_kscale(K)
    fr = mx_kscale(R)
    fl = mx_kscale(L)
    xtp = pack_weight(n((K, T)) / fk[:, None], "e2m1")
    xop = pack_weight(n((K, Z)) / fk[:, None], "e4m3")
    wp = pack_weight(n((K, R)) * 1 / np.sqrt(K) * fk[:, None] * fr, "e4m3")
    w2p = pack_weight(n((K, R)) * 1 / np.sqrt(K) * fk[:, None] * fr, "e5m2")
    wbp = pack_weight(n((R, N)) * 1 / np.sqrt(R) / fr[:, None], "e2m1")
    sxp = pack_weight(n((L, J)) / fl[:, None], "e4m3")
    wsp = pack_weight(n((L, N)) * 1 / np.sqrt(L) * fl[:, None], "e4m3")
    return {
        "xt_words": xtp[0],
        "xt_scales": xtp[1],
        "xo_words": xop[0],
        "xo_scales": xop[1],
        "w_words": wp[0],
        "w_scales": wp[1],
        "w2_words": w2p[0],
        "w2_scales": w2p[1],
        "wb_words": wbp[0],
        "wb_scales": wbp[1],
        "sx_words": sxp[0],
        "sx_scales": sxp[1],
        "ws_words": wsp[0],
        "ws_scales": wsp[1],
        "offs": striped(idx),
        "offs2": striped(idx2),
        "offs3": striped(idx3),
    }


def reference(xt_words, xt_scales, xo_words, xo_scales, w_words, w_scales, w2_words, w2_scales, wb_words, wb_scales, sx_words, sx_scales, ws_words, ws_scales, offs, offs2, offs3):
    idx = unstriped(offs)
    idx2 = unstriped(offs2)
    idx3 = unstriped(offs3)
    xtu = unpack_weight(xt_words, xt_scales, "e2m1")
    xou = unpack_weight(xo_words, xo_scales, "e4m3")
    wu = unpack_weight(w_words, w_scales, "e4m3")
    w2u = unpack_weight(w2_words, w2_scales, "e5m2")
    wbu = unpack_weight(wb_words, wb_scales, "e2m1")
    sxu = unpack_weight(sx_words, sx_scales, "e4m3")
    wsu = unpack_weight(ws_words, ws_scales, "e4m3")
    xtidxg = xtu[:, idx]
    xoidx2g = xou[:, idx2]
    a = wu.T @ xtidxg + w2u.T @ xoidx2g
    b = w2u.T @ xtidxg + wu.T @ xoidx2g
    hid = np.maximum(a, b)
    hidq = mxq(hid, 0, "e5m2")
    p = wbu.T @ hidq + wsu.T @ sxu
    y = np.zeros((N, E))
    y[:, idx3] = p
    return y

@@ -1,0 +1,209 @@
+from contextlib import ExitStack
+
+import concourse.mybir as mybir
+
+K, T, Z, J, R, N, L, E = 512, 1024, 1024, 256, 512, 256, 512, 1024
+FLOPS = 2 * (4 * K * R * J + R * N * J + L * N * J)
+
+F32 = mybir.dt.float32
+BF16 = mybir.dt.bfloat16
+I32 = mybir.dt.int32
+U32 = mybir.dt.uint32
+U16 = mybir.dt.uint16
+U8 = mybir.dt.uint8
+E4M3 = mybir.dt.float8_e4m3fn_x4
+E5M2 = mybir.dt.float8_e5m2_x4
+E2M1 = mybir.dt.float4_e2m1fn_x4
+MAX = mybir.AluOpType.max
+COPY = mybir.ActivationFunctionType.Copy
+
+P = 128
+PACK = 4
+HALF = 128
+HALVES = J // HALF
+LIST_COLS = HALF // 16
+
+
+def load_scales_low(queue, plane, scales):
+    queue.dma_start(out=plane[0:16, :].bitcast(I32), in_=scales[0].bitcast(I32))
+
+
+def load_scales_high(queue, plane, scales):
+    rows = scales[0, 2:16, :].bitcast(I32)
+    queue.dma_start(out=plane[16:P, :].bitcast(I32), in_=rows.unsqueeze(0).broadcast_to([8, 14, rows.shape[1]]))
+
+
+def load_words4(queue, tile, words):
+    queue.dma_start(out=tile[:].bitcast(I32), in_=words[0].rearrange("p c t -> p (c t)").bitcast(I32))
+
+
+def load_words2(queue, tile, words):
+    queue.dma_start(out=tile[:].bitcast(I32), in_=words[0].bitcast(I32))
+
+
+def tile_list_crossed_direct_skip_scattered_kernel(
+    tc, xt_words, xt_scales, xo_words, xo_scales, w_words, w_scales, w2_words, w2_scales,
+    wb_words, wb_scales, sx_words, sx_scales, ws_words, ws_scales, offs, offs2, offs3, out,
+):
+    nc = tc.nc
+    with ExitStack() as ctx:
+        sb = ctx.enter_context(tc.tile_pool(name="sb", bufs=1))
+        ps = ctx.enter_context(tc.psum_pool(name="ps", bufs=1))
+
+        def tile(name, cols, dtype):
+            return sb.tile([P, cols], dtype, name=name, align_bytes=64)
+
+        list_t = sb.tile([P, J // 16], U16, name="list_t")
+        list_o = sb.tile([P, J // 16], U16, name="list_o")
+        list_e = sb.tile([P, J // 16], U16, name="list_e")
+        xt_w, xt_s = tile("xt_w", T, U16), tile("xt_s", T, U8)
+        xo_w, xo_s = tile("xo_w", Z, U32), tile("xo_s", Z, U8)
+        w_raw, w_raw_s = tile("w_raw", R, U32), tile("w_raw_s", R, U8)
+        w2_raw, w2_raw_s = tile("w2_raw", R, U32), tile("w2_raw_s", R, U8)
+        wb_w, wb_s = tile("wb_w", 2 * N, U8), tile("wb_s", N, U8)
+        sx_w, sx_s = tile("sx_w", J, U32), tile("sx_s", J, U8)
+        ws_w, ws_s = tile("ws_w", N, U32), tile("ws_s", N, U8)
+
+        nc.sync.dma_start(list_t[:], offs)
+        load_scales_high(nc.scalar, xt_s, xt_scales)
+        load_scales_high(nc.gpsimd, w_raw_s, w_scales)
+        load_words2(nc.sync, xt_w, xt_words)
+        load_words4(nc.sync, w_raw, w_words)
+        load_scales_low(nc.sync, xt_s, xt_scales)
+        load_scales_low(nc.sync, w_raw_s, w_scales)
+        load_words4(nc.sync, w2_raw, w2_words)
+        load_words4(nc.sync, xo_w, xo_words)
+        load_scales_high(nc.gpsimd, w2_raw_s, w2_scales)
+        load_scales_low(nc.sync, w2_raw_s, w2_scales)
+        nc.sync.dma_start(list_o[:], offs2)
+        load_scales_high(nc.gpsimd, xo_s, xo_scales)
+        load_scales_low(nc.sync, xo_s, xo_scales)
+        load_words2(nc.sync, wb_w, wb_words)
+        load_scales_low(nc.sync, wb_s, wb_scales)
+        load_scales_high(nc.sync, wb_s, wb_scales)
+        load_words4(nc.sync, ws_w, ws_words)
+        load_scales_low(nc.sync, ws_s, ws_scales)
+        load_scales_high(nc.sync, ws_s, ws_scales)
+        load_scales_high(nc.gpsimd, sx_s, sx_scales)
+        load_words4(nc.sync, sx_w, sx_words)
+        load_scales_low(nc.sync, sx_s, sx_scales)
+        nc.sync.dma_start(list_e[:], offs3)
+
+        pages = [tile("page%d" % n, E, F32) for n in range(N // P)]
+        for page in pages:
+            nc.vector.memset(page[:], 0.0)
+
+        def gather(name, window, lst, h, dtype):
+            picked = tile("%s%d" % (name, h), HALF, dtype)
+            nc.vector.tensor_copy(out=picked[:], in_=window[:].indirect(lst[:, h * LIST_COLS : (h + 1) * LIST_COLS]))
+            return picked
+
+        def dealt(t):
+            return t[:].rearrange("p (t m) -> p m t", t=PACK)
+
+        def plain(t):
+            return t[:].rearrange("p (m t) -> p m t", t=PACK)
+
+        w_w, w_s = tile("w_w", R, U32), tile("w_s", R, U8)
+        w2_w, w2_s = tile("w2_w", R, U32), tile("w2_s", R, U8)
+
+        tok_w, tok_s, note_w, note_s = {}, {}, {}, {}
+        tok_w[0] = gather("tok_w", xt_w, list_t, 0, U16)
+        tok_s[0] = gather("tok_s", xt_s, list_t, 0, U8)
+        nc.scalar.copy(out=dealt(w_w), in_=plain(w_raw))
+        nc.vector.tensor_copy(out=dealt(w_s), in_=plain(w_raw_s))
+        tok_w[1] = gather("tok_w", xt_w, list_t, 1, U16)
+        tok_s[1] = gather("tok_s", xt_s, list_t, 1, U8)
+        nc.scalar.copy(out=dealt(w2_w), in_=plain(w2_raw))
+        nc.vector.tensor_copy(out=dealt(w2_s), in_=plain(w2_raw_s))
+        for h in range(HALVES):
+            note_w[h] = gather("note_w", xo_w, list_o, h, U32)
+            note_s[h] = gather("note_s", xo_s, list_o, h, U8)
+
+        first = (w_w, w_s, E4M3)
+        second = (w2_w, w2_s, E5M2)
+
+        def passes(bank, weight, words, scales, fmt, opens, closes):
+            ww, wsc, wfmt = weight
+            for t in range(PACK):
+                cols = slice(t * P, (t + 1) * P)
+                nc.tensor.matmul_mx(
+                    out=bank[:, t, :], lhsT=ww[:, cols].bitcast(wfmt), lhsT_scale=wsc[:, cols],
+                    rhs=words[:].bitcast(fmt), rhs_scale=scales[:],
+                    start=opens and t == 0, stop=closes and t == PACK - 1,
+                )
+
+        def tok_pass(bank, weight, h):
+            passes(bank, weight, tok_w[h], tok_s[h], E2M1, True, False)
+
+        def note_pass(bank, weight, h):
+            passes(bank, weight, note_w[h], note_s[h], E4M3, False, True)
+
+        def bank3(tag):
+            return ps.tile([P, PACK, HALF], F32, name=tag, tag=tag)
+
+        def take_a(bank, h):
+            a_sb = tile("a_sb%d" % h, PACK * HALF, F32)
+            nc.scalar.copy(out=plain(a_sb), in_=bank[:].rearrange("p t j -> p j t"))
+            return a_sb
+
+        def hidden(bank_b, a_sb, h):
+            hid = tile("hid%d" % h, PACK * HALF, BF16)
+            nc.vector.tensor_tensor(out=plain(hid), in0=bank_b[:].rearrange("p t j -> p j t"), in1=plain(a_sb), op=MAX)
+            codes, scales = tile("hid_w%d" % h, HALF, U32), tile("hid_s%d" % h, HALF, U8)
+            nc.vector.quantize_mx(out=codes[:].bitcast(E5M2), scales=scales[:], in_=hid[:])
+            return codes, scales
+
+        def hid_pass(bank, n, hq, opens, closes):
+            nc.tensor.matmul_mx(
+                out=bank[:, 0:HALF], lhsT=wb_w[:, 2 * n * P : 2 * (n + 1) * P].bitcast(E2M1), lhsT_scale=wb_s[:, n * P : (n + 1) * P],
+                rhs=hq[0][:].bitcast(E5M2), rhs_scale=hq[1][:], start=opens, stop=closes,
+            )
+
+        def own_pass(bank, n, h, opens, closes):
+            cols, slots = slice(n * P, (n + 1) * P), slice(h * HALF, (h + 1) * HALF)
+            nc.tensor.matmul_mx(
+                out=bank[:, 0:HALF], lhsT=ws_w[:, cols].bitcast(E4M3), lhsT_scale=ws_s[:, cols],
+                rhs=sx_w[:, slots].bitcast(E4M3), rhs_scale=sx_s[:, slots], start=opens, stop=closes,
+            )
+
+        def places(n, h):
+            return pages[n][:].indirect(list_e[:, h * LIST_COLS : (h + 1) * LIST_COLS])
+
+        def bank2(name, tag):
+            return ps.tile([P, PACK * HALF], F32, name=name, tag=tag)
+
+        a0, b0, a1, b1 = bank3("a0"), bank3("b0"), bank3("a1"), bank3("b1")
+        tok_pass(a0, first, 0)
+        tok_pass(a1, first, 1)
+        tok_pass(b0, second, 0)
+        tok_pass(b1, second, 1)
+        note_pass(a0, second, 0)
+        note_pass(b0, first, 0)
+        note_pass(a1, second, 1)
+        note_pass(b1, first, 1)
+        a_sb0 = take_a(a0, 0)
+        a_sb1 = take_a(a1, 1)
+        hq0 = hidden(b0, a_sb0, 0)
+        hq1 = hidden(b1, a_sb1, 1)
+        p0 = [bank2("p0%d" % n, "p0%d" % n) for n in range(2)]
+        for n in range(2):
+            hid_pass(p0[n], n, hq0, True, False)
+            own_pass(p0[n], n, 0, False, True)
+        p1 = [bank2("p10", "a0"), bank2("p11", "b0")]
+        for n in range(2):
+            own_pass(p1[n], n, 1, True, False)
+        for n in range(2):
+            hid_pass(p1[n], n, hq1, False, True)
+        p_sb0 = [tile("p_sb0%d" % n, HALF, F32) for n in range(2)]
+        p_sb1 = [tile("p_sb1%d" % n, HALF, F32) for n in range(2)]
+        for n in (1, 0):
+            nc.scalar.copy(out=p_sb0[n][:], in_=p0[n][:, 0:HALF])
+        nc.scalar.activation(out=places(0, 0), in_=p_sb0[0][:], func=COPY)
+        nc.vector.tensor_copy(out=places(1, 0), in_=p_sb0[1][:])
+        nc.scalar.copy(out=p_sb1[0][:], in_=p1[0][:, 0:HALF])
+        nc.vector.tensor_copy(out=p_sb1[1][:], in_=p1[1][:, 0:HALF])
+        nc.scalar.activation(out=places(0, 1), in_=p_sb1[0][:], func=COPY)
+        nc.vector.tensor_copy(out=places(1, 1), in_=p_sb1[1][:])
+        nc.scalar.dma_start(out=out[0:P, :], in_=pages[0][:])
+        nc.sync.dma_start(out=out[P : 2 * P, :], in_=pages[1][:])

@@ -65,26 +65,26 @@ def tile_list_crossed_direct_skip_scattered_kernel(
         ws_w, ws_s = tile("ws_w", N, U32), tile("ws_s", N, U8)
 
         nc.sync.dma_start(list_t[:], offs)
-        load_scales_high(nc.scalar, xt_s, xt_scales)
-        load_scales_high(nc.gpsimd, w_raw_s, w_scales)
-        load_words2(nc.sync, xt_w, xt_words)
-        load_words4(nc.sync, w_raw, w_words)
+        load_words2(nc.scalar, xt_w, xt_words)
+        load_scales_high(nc.sync, xt_s, xt_scales)
+        load_words4(nc.scalar, w_raw, w_words)
+        load_words4(nc.scalar, w2_raw, w2_words)
+        load_words4(nc.scalar, xo_w, xo_words)
+        load_scales_high(nc.gpsimd, xo_s, xo_scales)
         load_scales_low(nc.sync, xt_s, xt_scales)
+        load_scales_high(nc.sync, w_raw_s, w_scales)
         load_scales_low(nc.sync, w_raw_s, w_scales)
-        load_words4(nc.sync, w2_raw, w2_words)
-        load_words4(nc.sync, xo_w, xo_words)
-        load_scales_high(nc.gpsimd, w2_raw_s, w2_scales)
+        load_scales_high(nc.sync, w2_raw_s, w2_scales)
         load_scales_low(nc.sync, w2_raw_s, w2_scales)
         nc.sync.dma_start(list_o[:], offs2)
-        load_scales_high(nc.gpsimd, xo_s, xo_scales)
         load_scales_low(nc.sync, xo_s, xo_scales)
         load_words2(nc.sync, wb_w, wb_words)
         load_scales_low(nc.sync, wb_s, wb_scales)
         load_scales_high(nc.sync, wb_s, wb_scales)
+        load_scales_high(nc.gpsimd, ws_s, ws_scales)
+        load_scales_high(nc.gpsimd, sx_s, sx_scales)
         load_words4(nc.sync, ws_w, ws_words)
         load_scales_low(nc.sync, ws_s, ws_scales)
-        load_scales_high(nc.sync, ws_s, ws_scales)
-        load_scales_high(nc.gpsimd, sx_s, sx_scales)
         load_words4(nc.sync, sx_w, sx_words)
         load_scales_low(nc.sync, sx_s, sx_scales)
         nc.sync.dma_start(list_e[:], offs3)
@@ -98,8 +98,14 @@ def tile_list_crossed_direct_skip_scattered_kernel(
             nc.vector.tensor_copy(out=picked[:], in_=window[:].indirect(lst[:, h * LIST_COLS : (h + 1) * LIST_COLS]))
             return picked
 
-        def dealt(t):
-            return t[:].rearrange("p (t m) -> p m t", t=PACK)
+        def deal_words(dst, src):
+            nc.scalar.copy(
+                out=dst[:].rearrange("p (t c i) -> p c t i", t=PACK, i=PACK),
+                in_=src[:].rearrange("p (c i t) -> p c t i", t=PACK, i=PACK),
+            )
+
+        def deal_bytes(dst, src):
+            nc.vector.tensor_copy(out=dst[:].rearrange("p (t m) -> p t m", t=PACK), in_=src[:].rearrange("p (m t) -> p t m", t=PACK))
 
         def plain(t):
             return t[:].rearrange("p (m t) -> p m t", t=PACK)
@@ -110,12 +116,12 @@ def tile_list_crossed_direct_skip_scattered_kernel(
         tok_w, tok_s, note_w, note_s = {}, {}, {}, {}
         tok_w[0] = gather("tok_w", xt_w, list_t, 0, U16)
         tok_s[0] = gather("tok_s", xt_s, list_t, 0, U8)
-        nc.scalar.copy(out=dealt(w_w), in_=plain(w_raw))
-        nc.vector.tensor_copy(out=dealt(w_s), in_=plain(w_raw_s))
+        deal_words(w_w, w_raw)
+        deal_bytes(w_s, w_raw_s)
         tok_w[1] = gather("tok_w", xt_w, list_t, 1, U16)
         tok_s[1] = gather("tok_s", xt_s, list_t, 1, U8)
-        nc.scalar.copy(out=dealt(w2_w), in_=plain(w2_raw))
-        nc.vector.tensor_copy(out=dealt(w2_s), in_=plain(w2_raw_s))
+        deal_words(w2_w, w2_raw)
+        deal_bytes(w2_s, w2_raw_s)
         for h in range(HALVES):
             note_w[h] = gather("note_w", xo_w, list_o, h, U32)
             note_s[h] = gather("note_s", xo_s, list_o, h, U8)
@@ -197,7 +203,7 @@ def tile_list_crossed_direct_skip_scattered_kernel(
             hid_pass(p1[n], n, hq1, False, True)
         p_sb0 = [tile("p_sb0%d" % n, HALF, F32) for n in range(2)]
         p_sb1 = [tile("p_sb1%d" % n, HALF, F32) for n in range(2)]
-        for n in (1, 0):
+        for n in range(2):
             nc.scalar.copy(out=p_sb0[n][:], in_=p0[n][:, 0:HALF])
         nc.scalar.activation(out=places(0, 0), in_=p_sb0[0][:], func=COPY)
         nc.vector.tensor_copy(out=places(1, 0), in_=p_sb0[1][:])

@@ -33,6 +33,10 @@ def load_scales_high(queue, plane, scales):
     queue.dma_start(out=plane[16:P, :].bitcast(I32), in_=rows.unsqueeze(0).broadcast_to([8, 14, rows.shape[1]]))
 
 
+def load_scales_quadrant(queue, plane, scales, q):
+    queue.dma_start(out=plane[32 * q : 32 * q + 4, :].bitcast(I32), in_=scales[0, 4 * q : 4 * q + 4, :].bitcast(I32))
+
+
 def load_words4(queue, tile, words):
     queue.dma_start(out=tile[:].bitcast(I32), in_=words[0].rearrange("p c t -> p (c t)").bitcast(I32))
 
@@ -64,34 +68,35 @@ def tile_list_crossed_direct_skip_scattered_kernel(
         sx_w, sx_s = tile("sx_w", J, U32), tile("sx_s", J, U8)
         ws_w, ws_s = tile("ws_w", N, U32), tile("ws_s", N, U8)
 
+        load_scales_low(nc.scalar, xt_s, xt_scales)
         nc.sync.dma_start(list_t[:], offs)
-        load_words2(nc.scalar, xt_w, xt_words)
-        load_scales_high(nc.sync, xt_s, xt_scales)
+        load_scales_low(nc.scalar, w_raw_s, w_scales)
+        load_words2(nc.sync, xt_w, xt_words)
         load_words4(nc.scalar, w_raw, w_words)
-        load_words4(nc.scalar, w2_raw, w2_words)
-        load_words4(nc.scalar, xo_w, xo_words)
-        load_scales_high(nc.gpsimd, xo_s, xo_scales)
-        load_scales_low(nc.sync, xt_s, xt_scales)
         load_scales_high(nc.sync, w_raw_s, w_scales)
-        load_scales_low(nc.sync, w_raw_s, w_scales)
+        load_scales_high(nc.scalar, xt_s, xt_scales)
         load_scales_high(nc.sync, w2_raw_s, w2_scales)
+        load_scales_high(nc.gpsimd, xo_s, xo_scales)
         load_scales_low(nc.sync, w2_raw_s, w2_scales)
         nc.sync.dma_start(list_o[:], offs2)
         load_scales_low(nc.sync, xo_s, xo_scales)
+        load_words4(nc.sync, w2_raw, w2_words)
+        load_words4(nc.sync, xo_w, xo_words)
+        load_scales_high(nc.gpsimd, wb_s, wb_scales)
         load_words2(nc.sync, wb_w, wb_words)
         load_scales_low(nc.sync, wb_s, wb_scales)
-        load_scales_high(nc.sync, wb_s, wb_scales)
-        load_scales_high(nc.gpsimd, ws_s, ws_scales)
-        load_scales_high(nc.gpsimd, sx_s, sx_scales)
         load_words4(nc.sync, ws_w, ws_words)
         load_scales_low(nc.sync, ws_s, ws_scales)
+        load_scales_high(nc.sync, ws_s, ws_scales)
+        load_scales_high(nc.sync, sx_s, sx_scales)
         load_words4(nc.sync, sx_w, sx_words)
         load_scales_low(nc.sync, sx_s, sx_scales)
         nc.sync.dma_start(list_e[:], offs3)
 
         pages = [tile("page%d" % n, E, F32) for n in range(N // P)]
         for page in pages:
-            nc.vector.memset(page[:], 0.0)
+            nc.vector.memset(page[:, : E // 2 - 1], 0.0)
+            nc.vector.memset(page[:, E // 2 - 1 :], 0.0)
 
         def gather(name, window, lst, h, dtype):
             picked = tile("%s%d" % (name, h), HALF, dtype)
@@ -114,17 +119,18 @@ def tile_list_crossed_direct_skip_scattered_kernel(
         w2_w, w2_s = tile("w2_w", R, U32), tile("w2_s", R, U8)
 
         tok_w, tok_s, note_w, note_s = {}, {}, {}, {}
-        tok_w[0] = gather("tok_w", xt_w, list_t, 0, U16)
-        tok_s[0] = gather("tok_s", xt_s, list_t, 0, U8)
+        for h in range(HALVES):
+            tok_w[h] = gather("tok_w", xt_w, list_t, h, U16)
         deal_words(w_w, w_raw)
         deal_bytes(w_s, w_raw_s)
-        tok_w[1] = gather("tok_w", xt_w, list_t, 1, U16)
-        tok_s[1] = gather("tok_s", xt_s, list_t, 1, U8)
+        for h in range(HALVES):
+            tok_s[h] = gather("tok_s", xt_s, list_t, h, U8)
         deal_words(w2_w, w2_raw)
         deal_bytes(w2_s, w2_raw_s)
         for h in range(HALVES):
-            note_w[h] = gather("note_w", xo_w, list_o, h, U32)
             note_s[h] = gather("note_s", xo_s, list_o, h, U8)
+        for h in range(HALVES):
+            note_w[h] = gather("note_w", xo_w, list_o, h, U32)
 
         first = (w_w, w_s, E4M3)
         second = (w2_w, w2_s, E5M2)
@@ -154,7 +160,7 @@ def tile_list_crossed_direct_skip_scattered_kernel(
             return a_sb
 
         def hidden(bank_b, a_sb, h):
-            hid = tile("hid%d" % h, PACK * HALF, BF16)
+            hid = sb.tile([P, PACK * HALF], BF16, name="hid%d" % h, tag="hid", align_bytes=64)
             nc.vector.tensor_tensor(out=plain(hid), in0=bank_b[:].rearrange("p t j -> p j t"), in1=plain(a_sb), op=MAX)
             codes, scales = tile("hid_w%d" % h, HALF, U32), tile("hid_s%d" % h, HALF, U8)
             nc.vector.quantize_mx(out=codes[:].bitcast(E5M2), scales=scales[:], in_=hid[:])
@@ -192,24 +198,22 @@ def tile_list_crossed_direct_skip_scattered_kernel(
         a_sb1 = take_a(a1, 1)
         hq0 = hidden(b0, a_sb0, 0)
         hq1 = hidden(b1, a_sb1, 1)
-        p0 = [bank2("p0%d" % n, "p0%d" % n) for n in range(2)]
-        for n in range(2):
-            hid_pass(p0[n], n, hq0, True, False)
-            own_pass(p0[n], n, 0, False, True)
-        p1 = [bank2("p10", "a0"), bank2("p11", "b0")]
-        for n in range(2):
-            own_pass(p1[n], n, 1, True, False)
-        for n in range(2):
-            hid_pass(p1[n], n, hq1, False, True)
-        p_sb0 = [tile("p_sb0%d" % n, HALF, F32) for n in range(2)]
-        p_sb1 = [tile("p_sb1%d" % n, HALF, F32) for n in range(2)]
-        for n in range(2):
-            nc.scalar.copy(out=p_sb0[n][:], in_=p0[n][:, 0:HALF])
-        nc.scalar.activation(out=places(0, 0), in_=p_sb0[0][:], func=COPY)
-        nc.vector.tensor_copy(out=places(1, 0), in_=p_sb0[1][:])
-        nc.scalar.copy(out=p_sb1[0][:], in_=p1[0][:, 0:HALF])
-        nc.vector.tensor_copy(out=p_sb1[1][:], in_=p1[1][:, 0:HALF])
-        nc.scalar.activation(out=places(0, 1), in_=p_sb1[0][:], func=COPY)
-        nc.vector.tensor_copy(out=places(1, 1), in_=p_sb1[1][:])
-        nc.scalar.dma_start(out=out[0:P, :], in_=pages[0][:])
-        nc.sync.dma_start(out=out[P : 2 * P, :], in_=pages[1][:])
+        p0 = [bank2("p00", "a0"), bank2("p01", "b0")]
+        p1 = [bank2("p10", "a1"), bank2("p11", "b1")]
+        for h, (banks, hq) in enumerate(((p0, hq0), (p1, hq1))):
+            for n in range(2):
+                own_pass(banks[n], n, h, True, False)
+            for n in range(2):
+                hid_pass(banks[n], n, hq, False, True)
+        p_sb00, p_sb10, p_sb11 = tile("p_sb00", HALF, F32), tile("p_sb10", HALF, F32), tile("p_sb11", HALF, F32)
+        p_sb01 = sb.tile([P, HALF], F32, name="p_sb01", tag="hid", align_bytes=64)
+        nc.scalar.copy(out=p_sb00[:], in_=p0[0][:, 0:HALF])
+        nc.scalar.activation(out=places(0, 0), in_=p_sb00[:], func=COPY)
+        nc.vector.tensor_copy(out=p_sb01[:], in_=p0[1][:, 0:HALF])
+        nc.scalar.activation(out=places(1, 0), in_=p_sb01[:], func=COPY)
+        nc.vector.tensor_copy(out=p_sb10[:], in_=p1[0][:, 0:HALF])
+        nc.vector.tensor_copy(out=p_sb11[:], in_=p1[1][:, 0:HALF])
+        nc.vector.tensor_copy(out=places(0, 1), in_=p_sb10[:])
+        nc.sync.dma_start(out=out[0:P, :], in_=pages[0][:])
+        nc.scalar.activation(out=places(1, 1), in_=p_sb11[:], func=COPY)
+        nc.scalar.dma_start(out=out[P : 2 * P, :], in_=pages[1][:])

@@ -83,11 +83,11 @@ def tile_list_crossed_direct_skip_scattered_kernel(
         load_words4(nc.sync, w2_raw, w2_words)
         load_words4(nc.sync, xo_w, xo_words)
         load_scales_high(nc.gpsimd, wb_s, wb_scales)
+        load_scales_high(nc.gpsimd, ws_s, ws_scales)
         load_words2(nc.sync, wb_w, wb_words)
         load_scales_low(nc.sync, wb_s, wb_scales)
         load_words4(nc.sync, ws_w, ws_words)
         load_scales_low(nc.sync, ws_s, ws_scales)
-        load_scales_high(nc.sync, ws_s, ws_scales)
         load_scales_high(nc.sync, sx_s, sx_scales)
         load_words4(nc.sync, sx_w, sx_words)
         load_scales_low(nc.sync, sx_s, sx_scales)

from contextlib import ExitStack

import concourse.mybir as mybir

K, T, Z, J, R, N, L, E = 512, 1024, 1024, 256, 512, 256, 512, 1024
FLOPS = 2 * (4 * K * R * J + R * N * J + L * N * J)

F32 = mybir.dt.float32
BF16 = mybir.dt.bfloat16
I32 = mybir.dt.int32
U32 = mybir.dt.uint32
U16 = mybir.dt.uint16
U8 = mybir.dt.uint8
E4M3 = mybir.dt.float8_e4m3fn_x4
E5M2 = mybir.dt.float8_e5m2_x4
E2M1 = mybir.dt.float4_e2m1fn_x4
MAX = mybir.AluOpType.max
COPY = mybir.ActivationFunctionType.Copy

P = 128
PACK = 4
HALF = 128
HALVES = J // HALF
LIST_COLS = HALF // 16


def load_scales_low(queue, plane, scales):
    queue.dma_start(out=plane[0:16, :].bitcast(I32), in_=scales[0].bitcast(I32))


def load_scales_high(queue, plane, scales):
    rows = scales[0, 2:16, :].bitcast(I32)
    queue.dma_start(out=plane[16:P, :].bitcast(I32), in_=rows.unsqueeze(0).broadcast_to([8, 14, rows.shape[1]]))


def load_scales_quadrant(queue, plane, scales, q):
    queue.dma_start(out=plane[32 * q : 32 * q + 4, :].bitcast(I32), in_=scales[0, 4 * q : 4 * q + 4, :].bitcast(I32))


def load_words4(queue, tile, words):
    queue.dma_start(out=tile[:].bitcast(I32), in_=words[0].rearrange("p c t -> p (c t)").bitcast(I32))


def load_words2(queue, tile, words):
    queue.dma_start(out=tile[:].bitcast(I32), in_=words[0].bitcast(I32))


def tile_list_crossed_direct_skip_scattered_kernel(
    tc, xt_words, xt_scales, xo_words, xo_scales, w_words, w_scales, w2_words, w2_scales,
    wb_words, wb_scales, sx_words, sx_scales, ws_words, ws_scales, offs, offs2, offs3, out,
):
    nc = tc.nc
    with ExitStack() as ctx:
        sb = ctx.enter_context(tc.tile_pool(name="sb", bufs=1))
        ps = ctx.enter_context(tc.psum_pool(name="ps", bufs=1))

        def tile(name, cols, dtype):
            return sb.tile([P, cols], dtype, name=name, align_bytes=64)

        list_t = sb.tile([P, J // 16], U16, name="list_t")
        list_o = sb.tile([P, J // 16], U16, name="list_o")
        list_e = sb.tile([P, J // 16], U16, name="list_e")
        xt_w, xt_s = tile("xt_w", T, U16), tile("xt_s", T, U8)
        xo_w, xo_s = tile("xo_w", Z, U32), tile("xo_s", Z, U8)
        w_raw, w_raw_s = tile("w_raw", R, U32), tile("w_raw_s", R, U8)
        w2_raw, w2_raw_s = tile("w2_raw", R, U32), tile("w2_raw_s", R, U8)
        wb_w, wb_s = tile("wb_w", 2 * N, U8), tile("wb_s", N, U8)
        sx_w, sx_s = tile("sx_w", J, U32), tile("sx_s", J, U8)
        ws_w, ws_s = tile("ws_w", N, U32), tile("ws_s", N, U8)

        load_scales_low(nc.scalar, xt_s, xt_scales)
        nc.sync.dma_start(list_t[:], offs)
        load_scales_low(nc.scalar, w_raw_s, w_scales)
        load_words2(nc.sync, xt_w, xt_words)
        load_words4(nc.scalar, w_raw, w_words)
        load_scales_high(nc.sync, w_raw_s, w_scales)
        load_scales_high(nc.scalar, xt_s, xt_scales)
        load_scales_high(nc.sync, w2_raw_s, w2_scales)
        load_scales_high(nc.gpsimd, xo_s, xo_scales)
        load_scales_low(nc.sync, w2_raw_s, w2_scales)
        nc.sync.dma_start(list_o[:], offs2)
        load_scales_low(nc.sync, xo_s, xo_scales)
        load_words4(nc.sync, w2_raw, w2_words)
        load_words4(nc.sync, xo_w, xo_words)
        load_scales_high(nc.gpsimd, wb_s, wb_scales)
        load_scales_high(nc.gpsimd, ws_s, ws_scales)
        load_words2(nc.sync, wb_w, wb_words)
        load_scales_low(nc.sync, wb_s, wb_scales)
        load_words4(nc.sync, ws_w, ws_words)
        load_scales_low(nc.sync, ws_s, ws_scales)
        load_scales_high(nc.sync, sx_s, sx_scales)
        load_words4(nc.sync, sx_w, sx_words)
        load_scales_low(nc.sync, sx_s, sx_scales)
        nc.sync.dma_start(list_e[:], offs3)

        pages = [tile("page%d" % n, E, F32) for n in range(N // P)]
        for page in pages:
            nc.vector.memset(page[:, : E // 2 - 1], 0.0)
            nc.vector.memset(page[:, E // 2 - 1 :], 0.0)

        def gather(name, window, lst, h, dtype):
            picked = tile("%s%d" % (name, h), HALF, dtype)
            nc.vector.tensor_copy(out=picked[:], in_=window[:].indirect(lst[:, h * LIST_COLS : (h + 1) * LIST_COLS]))
            return picked

        def deal_words(dst, src):
            nc.scalar.copy(
                out=dst[:].rearrange("p (t c i) -> p c t i", t=PACK, i=PACK),
                in_=src[:].rearrange("p (c i t) -> p c t i", t=PACK, i=PACK),
            )

        def deal_bytes(dst, src):
            nc.vector.tensor_copy(out=dst[:].rearrange("p (t m) -> p t m", t=PACK), in_=src[:].rearrange("p (m t) -> p t m", t=PACK))

        def plain(t):
            return t[:].rearrange("p (m t) -> p m t", t=PACK)

        w_w, w_s = tile("w_w", R, U32), tile("w_s", R, U8)
        w2_w, w2_s = tile("w2_w", R, U32), tile("w2_s", R, U8)

        tok_w, tok_s, note_w, note_s = {}, {}, {}, {}
        for h in range(HALVES):
            tok_w[h] = gather("tok_w", xt_w, list_t, h, U16)
        deal_words(w_w, w_raw)
        deal_bytes(w_s, w_raw_s)
        for h in range(HALVES):
            tok_s[h] = gather("tok_s", xt_s, list_t, h, U8)
        deal_words(w2_w, w2_raw)
        deal_bytes(w2_s, w2_raw_s)
        for h in range(HALVES):
            note_s[h] = gather("note_s", xo_s, list_o, h, U8)
        for h in range(HALVES):
            note_w[h] = gather("note_w", xo_w, list_o, h, U32)

        first = (w_w, w_s, E4M3)
        second = (w2_w, w2_s, E5M2)

        def passes(bank, weight, words, scales, fmt, opens, closes):
            ww, wsc, wfmt = weight
            for t in range(PACK):
                cols = slice(t * P, (t + 1) * P)
                nc.tensor.matmul_mx(
                    out=bank[:, t, :], lhsT=ww[:, cols].bitcast(wfmt), lhsT_scale=wsc[:, cols],
                    rhs=words[:].bitcast(fmt), rhs_scale=scales[:],
                    start=opens and t == 0, stop=closes and t == PACK - 1,
                )

        def tok_pass(bank, weight, h):
            passes(bank, weight, tok_w[h], tok_s[h], E2M1, True, False)

        def note_pass(bank, weight, h):
            passes(bank, weight, note_w[h], note_s[h], E4M3, False, True)

        def bank3(tag):
            return ps.tile([P, PACK, HALF], F32, name=tag, tag=tag)

        def take_a(bank, h):
            a_sb = tile("a_sb%d" % h, PACK * HALF, F32)
            nc.scalar.copy(out=plain(a_sb), in_=bank[:].rearrange("p t j -> p j t"))
            return a_sb

        def hidden(bank_b, a_sb, h):
            hid = sb.tile([P, PACK * HALF], BF16, name="hid%d" % h, tag="hid", align_bytes=64)
            nc.vector.tensor_tensor(out=plain(hid), in0=bank_b[:].rearrange("p t j -> p j t"), in1=plain(a_sb), op=MAX)
            codes, scales = tile("hid_w%d" % h, HALF, U32), tile("hid_s%d" % h, HALF, U8)
            nc.vector.quantize_mx(out=codes[:].bitcast(E5M2), scales=scales[:], in_=hid[:])
            return codes, scales

        def hid_pass(bank, n, hq, opens, closes):
            nc.tensor.matmul_mx(
                out=bank[:, 0:HALF], lhsT=wb_w[:, 2 * n * P : 2 * (n + 1) * P].bitcast(E2M1), lhsT_scale=wb_s[:, n * P : (n + 1) * P],
                rhs=hq[0][:].bitcast(E5M2), rhs_scale=hq[1][:], start=opens, stop=closes,
            )

        def own_pass(bank, n, h, opens, closes):
            cols, slots = slice(n * P, (n + 1) * P), slice(h * HALF, (h + 1) * HALF)
            nc.tensor.matmul_mx(
                out=bank[:, 0:HALF], lhsT=ws_w[:, cols].bitcast(E4M3), lhsT_scale=ws_s[:, cols],
                rhs=sx_w[:, slots].bitcast(E4M3), rhs_scale=sx_s[:, slots], start=opens, stop=closes,
            )

        def places(n, h):
            return pages[n][:].indirect(list_e[:, h * LIST_COLS : (h + 1) * LIST_COLS])

        def bank2(name, tag):
            return ps.tile([P, PACK * HALF], F32, name=name, tag=tag)

        a0, b0, a1, b1 = bank3("a0"), bank3("b0"), bank3("a1"), bank3("b1")
        tok_pass(a0, first, 0)
        tok_pass(a1, first, 1)
        tok_pass(b0, second, 0)
        tok_pass(b1, second, 1)
        note_pass(a0, second, 0)
        note_pass(b0, first, 0)
        note_pass(a1, second, 1)
        note_pass(b1, first, 1)
        a_sb0 = take_a(a0, 0)
        a_sb1 = take_a(a1, 1)
        hq0 = hidden(b0, a_sb0, 0)
        hq1 = hidden(b1, a_sb1, 1)
        p0 = [bank2("p00", "a0"), bank2("p01", "b0")]
        p1 = [bank2("p10", "a1"), bank2("p11", "b1")]
        for h, (banks, hq) in enumerate(((p0, hq0), (p1, hq1))):
            for n in range(2):
                own_pass(banks[n], n, h, True, False)
            for n in range(2):
                hid_pass(banks[n], n, hq, False, True)
        p_sb00, p_sb10, p_sb11 = tile("p_sb00", HALF, F32), tile("p_sb10", HALF, F32), tile("p_sb11", HALF, F32)
        p_sb01 = sb.tile([P, HALF], F32, name="p_sb01", tag="hid", align_bytes=64)
        nc.scalar.copy(out=p_sb00[:], in_=p0[0][:, 0:HALF])
        nc.scalar.activation(out=places(0, 0), in_=p_sb00[:], func=COPY)
        nc.vector.tensor_copy(out=p_sb01[:], in_=p0[1][:, 0:HALF])
        nc.scalar.activation(out=places(1, 0), in_=p_sb01[:], func=COPY)
        nc.vector.tensor_copy(out=p_sb10[:], in_=p1[0][:, 0:HALF])
        nc.vector.tensor_copy(out=p_sb11[:], in_=p1[1][:, 0:HALF])
        nc.vector.tensor_copy(out=places(0, 1), in_=p_sb10[:])
        nc.sync.dma_start(out=out[0:P, :], in_=pages[0][:])
        nc.scalar.activation(out=places(1, 1), in_=p_sb11[:], func=COPY)
        nc.scalar.dma_start(out=out[P : 2 * P, :], in_=pages[1][:])
